import numpy as np, ml_dtypes
CORES = [24,25,26,27,28,29,30,31]
N = 8
BF = ml_dtypes.bfloat16
def gentries(a):
    return np.ascontiguousarray(a.reshape(8, 16, -1).transpose(0, 2, 1)).reshape(8, -1)
def gtable(e):
    e = np.asarray(e); return np.ascontiguousarray(e.reshape(8, -1, 16).transpose(0, 2, 1)).reshape(128, -1).astype(np.int32)
W, K, O, TH, CAP, RO = 8192, 16, 256, 320, 16, 4
def ring(rng):
    gap = rng.integers(0, W // K, (N, 8, K, O)) + 1; gap[:, :, 0] = rng.integers(0, W, (N, 8, O))
    return np.add.accumulate(gap, axis=2) & (W - 1)
def held(c, want, pri):
    h = np.zeros(c.shape, np.int64)
    for q in range(N):
        for g in range(8):
            p = np.broadcast_to(pri[q, g], (K, O)); low = np.full(W, O); w = want[q, g]
            np.minimum.at(low, c[q, g][w], p[w]); h[q, g] = w & (low[c[q, g]] == p)
    return h
def crew(rng):
    c = ring(rng); lv = rng.choice(np.array([0, K // 2, K - 2, K - 1, K]), (8, O)); pri = np.zeros((8, O), np.int64); cls = np.zeros((8, 1, O), bool)
    nf = rng.permutation(8 + (O * 45 // 100 - 8) * np.arange(8) // 7)
    for g in range(8):
        n = int(nf[g]); o = rng.permutation(O); lv[g, o[:n]] = K; pri[g, o] = np.arange(O); cls[g, 0, o[:n]] = True
        for q in range(N):
            own = rng.permutation(W)[:n * K].reshape(K, n); c[q, g][:, o[:n]] = own
            rest = c[q, g][:, o[n:]]; t = rng.choice(own.reshape(-1), O - n); k = rng.integers(0, K, O - n)
            ok = (rng.random(O - n) < 0.3) & ~np.any(rest == t, axis=0)
            rest[k[ok], np.flatnonzero(ok)] = t[ok]; c[q, g][:, o[n:]] = rest
    want = (np.arange(K)[:, None] < lv[:, None, :]) & (cls | (rng.random((N, 8, K, O)) < 0.95))
    return c, held(c, want, np.broadcast_to(pri, (N, 8, O)))
def far(rng, m, share, over):
    k = rng.integers(0, K, (N, 8, O)); k = np.where(rng.random(k.shape) < 0.5, k, (K - 1) * rng.integers(0, 2, k.shape))
    hit = (rng.random((N, 8, 1, O)) < share) & (np.arange(K)[:, None] == k[:, :, None, :])
    return np.where(hit, TH + rng.integers(1, over + 1, m.shape), m)
def naps(rng, share):
    return np.add.reduce((rng.random((N, 8, O, RO)) < share).astype(np.int64) << np.arange(RO), axis=3)
def pack(x, c, h, m, wk, lump=None):
    ix = c.reshape(N, 8, 1, K * O); xc = np.take_along_axis(x, ix, 3); m = m.reshape(N, 8, 1, K * O)
    d = (m >> 4) + (((np.arange(16).reshape(16, 1) + ix) & 15) < (m & 15))
    if lump is not None:
        s = lump.reshape(N, 8, 1, K * O); i = (np.arange(16).reshape(16, 1) + s) & 15
        most = np.take_along_axis(np.maximum(xc, 255 - xc), i, 2).astype(np.int64); before = np.add.accumulate(most, axis=2) - most
        u = np.zeros(i.shape, np.int64); np.put_along_axis(u, i, np.minimum(np.maximum(m - before, 0), most), 2)
        d = np.where(s < 16, u, d)
    e = np.where(xc < 128, xc + d, xc - d)
    return {"x": np.ascontiguousarray(x.reshape(N, 128, W)).astype(np.float32).astype(BF), "snap": np.ascontiguousarray(e.reshape(N, 128, K * O)).astype(np.float32).astype(BF),
            "cs": np.stack([gtable(a.reshape(8, -1)) for a in c]), "hold": np.stack([gtable(a.reshape(8, -1)) for a in h]), "wake": np.stack([gtable(a) for a in wk])}
def cells(rng):
    return rng.integers(0, 256, (N, 8, 16, W), dtype=np.int32)
def setup_inputs(rng):
    x = cells(rng); c, h = crew(rng); m = far(rng, rng.integers(0, TH + 1, c.shape), 0.08, 600)
    return pack(x, c, h, m, naps(rng, rng.choice(np.array([0.5, 0.7, 0.9]), (N, 8, 1, 1))))
def setup_inputs_room(rng):
    x = cells(rng); c = np.zeros((N, 8, K, O), np.int64); h = np.ones((N, 8, K, O), np.int64); m = rng.integers(0, TH + 1, c.shape); wk = naps(rng, 0.7)
    cnt = rng.permutation(np.array([0, 1, CAP - 1, CAP, CAP + 1, 2 * CAP, O - 1, O]))
    for g in range(8):
        n = int(cnt[g]); o = rng.permutation(O)
        if n == 0: wk[:, g] = 1
        for q in range(N):
            c[q, g] = rng.permutation(W)[:K * O].reshape(K, O)
            rest = o[n:] if q & 1 else o[n:][rng.random(O - n) < 0.5]
            h[q, g][rng.integers(0, K, len(rest)), rest] = 0
            if q & 1 == 0 and n > 0: m[q, g][rng.integers(0, K), rest[rng.random(len(rest)) < 0.15]] = TH + 1
    return pack(x, c, h, m, wk)
def setup_inputs_storm(rng):
    x = cells(rng); c = ring(rng); m = rng.integers(0, TH + 1, c.shape); want = rng.random(c.shape) < 0.5; wk = naps(rng, 0.8)
    pri = np.argsort(rng.random((N, 8, O)), axis=-1); deal = rng.permutation(8); role = deal & 3
    for g in range(8):
        if deal[g] == 0:
            want[:, g] = True
            for q in range(N): c[q, g] = rng.permutation(W)[:K * O].reshape(K, O)
        if role[g] == 0: m[:, g, rng.integers(0, K)] = TH + 1 + rng.integers(0, 600, (N, O))
        if role[g] == 1: m[::2, g, 0, ::2] = TH + 1
        if role[g] == 2:
            o = int(rng.integers(0, O))
            for q in range(N):
                v = int(rng.integers(0, W)); k = rng.integers(0, K, O); ok = ~np.any(c[q, g] == v, axis=0)
                c[q, g][k[ok], np.flatnonzero(ok)] = v; x[q, g, :, v] = rng.integers(0, 16, 16) + 240 * (q & 1)
                want[q, g, :, o] = True; i = int(np.flatnonzero(pri[q, g] == 0)[0]); pri[q, g, i] = pri[q, g, o]; pri[q, g, o] = 0
        if role[g] == 3: want[:, g] = False; wk[:, g] = wk[:, g] & ~1
    p = 2 * int(rng.integers(0, N // 2)); m[p:p + 2] = far(rng, m, 1.0, 600)[p:p + 2]
    return pack(x, c, held(c, want, pri), m, wk)
def setup_inputs_crowd(rng):
    x = cells(rng); c = np.zeros((N, 8, K, O), np.int64)
    for q in range(N):
        for g in range(8):
            P = 64 if g & 1 else 256
            pool = rng.permutation(np.concatenate([np.array([0, W - 1]), 1 + rng.permutation(W - 2)[:P - 2]]))
            c[q, g] = pool[(rng.integers(0, P, O) + np.arange(K)[:, None] * (2 * rng.integers(0, P // 2, O) + 1)) & (P - 1)]
    pri = np.argsort(rng.random((8, O)), axis=-1); lv = np.where(pri < 3, K, rng.integers(0, K + 1, (8, O)))
    lv[rng.permutation(8)[:4]] = 0
    want = np.broadcast_to(np.arange(K)[:, None] < lv[:, None, :], (N, 8, K, O))
    m = far(rng, rng.integers(0, TH + 1, c.shape), 0.01, 600)
    return pack(x, c, held(c, want, np.broadcast_to(pri, (N, 8, O))), m, naps(rng, rng.choice(np.array([0.6, 1.0]), (N, 8, 1, 1))))
def setup_inputs_ties(rng):
    x = cells(rng); z = rng.random((N, 8, 1, W)); x = np.where(z < 0.06, 0, np.where(z < 0.12, 255, x)).astype(np.int32)
    c, h = crew(rng); m = far(rng, rng.choice(np.array([0, TH - 1, TH]), c.shape), 0.12, 1)
    wk = naps(rng, 0.75) & ~(1 << int(rng.integers(1, 3)))
    return pack(x, c, h, m, wk, np.minimum(rng.integers(0, 32, c.shape), 16))
def setup_inputs_spread(rng):
    x = np.minimum((np.exp2(8.01 * rng.random((N, 8, 1, W))) * rng.random((N, 8, 16, W))).astype(np.int32), 255)
    c, h = crew(rng); m = far(rng, (TH * rng.random(c.shape) ** 4).astype(np.int64), 0.1, 1000)
    share = np.ones((N, 1, 1, 1)) * rng.permutation(np.array([0.0, 0.2, 0.4, 0.6, 0.8, 0.9, 1.0, 1.0])).reshape(1, 8, 1, 1)
    return pack(x, c, h, m, naps(rng, share))
def check_inputs(d):
    bad = []
    for k in ("x", "snap"):
        v = np.asarray(d[k]).astype(np.float32)
        if not (np.all(v >= 0) and np.all(v <= 255) and np.all(v == np.floor(v))): bad.append("range of " + k)
    for k, hi in (("cs", W - 1), ("hold", 1), ("wake", 2 ** RO - 1)):
        if np.min(d[k]) < 0 or np.max(d[k]) > hi: bad.append("range of " + k)
    c = np.stack([gentries(a) for a in d["cs"]]).reshape(N, 8, K, O); h = np.stack([gentries(a) for a in d["hold"]]).reshape(N, 8, K, O)
    s = np.sort(c, axis=2)
    if np.any(s[:, :, 1:] == s[:, :, :-1]): bad.append("cells of an operation differ")
    for q in range(N):
        for g in range(8):
            v = c[q, g][h[q, g] == 1]
            if len(np.unique(v)) != len(v) and "a cell has one holder" not in bad: bad.append("a cell has one holder")
    return bad
def reference(x, snap, cs, hold, wake):
    v = np.zeros((N, 8, 16, W + 1), np.int32)
    v[..., :W] = x.astype(np.float32).astype(np.int32).reshape(N, 8, 16, W)
    e = snap.astype(np.float32).astype(np.int32).reshape(N, 8, 16, K * O)
    c = np.stack([gentries(a) for a in cs]).astype(np.int64).reshape(N, 8, K, O); h = np.stack([gentries(a) for a in hold]).reshape(N, 8, K, O)
    wk = np.stack([gentries(a) for a in wake]).astype(np.int64)
    own = np.arange(O) + 1; lane = np.broadcast_to(np.arange(O), (N, 8, O)); cur = np.array(lane)
    lock = np.zeros((N, 8, W + 1), np.int64)
    np.put_along_axis(lock, np.where(h == 1, c, W).reshape(N, 8, -1), np.broadcast_to(own, c.shape).reshape(N, 8, -1), 2)
    for t in range(RO):
        twin = np.arange(N) ^ (1 + t % (N - 1))
        got = np.take_along_axis(v, c.reshape(N, 8, 1, -1), 3)
        dist = np.add.reduce(np.abs(got - e), axis=2).reshape(N, 8, K, O)
        who = np.take_along_axis(lock, c.reshape(N, 8, -1), 2).reshape(N, 8, K, O); mine = who == own
        bad = np.any(dist > TH, axis=2); full = np.all(mine, axis=2)
        abort = bad | bad[twin]; ready = full & full[twin] & ~abort
        before = np.add.accumulate(ready.astype(np.int64), axis=2) - ready
        commit = ready & (before < CAP); done = abort | commit
        first = np.argmin(mine, axis=2)[:, :, None, :]
        cell = np.take_along_axis(np.take_along_axis(c, first, 2)[:, :, 0], cur, 2); by = np.take_along_axis(np.take_along_axis(who, first, 2)[:, :, 0], cur, 2)
        gone = np.take_along_axis(done, cur, 2); act = (((wk >> t) & 1) == 1) & ~gone & ~np.take_along_axis(full, cur, 2)
        np.put_along_axis(lock, np.where(done[:, :, None, :] & mine, c, W).reshape(N, 8, -1), 0, 2)
        for q in range(N):
            for g in range(8):
                w = np.flatnonzero(act[q, g] & (by[q, g] == 0)); low = np.full(W, O); a = cell[q, g][w]
                np.minimum.at(low, a, w); win = low[a] == w
                lock[q, g][a[win]] = cur[q, g][w[win]] + 1
        cur = np.where(gone, lane, np.where(act & (by > 0), by - 1, cur))
        cm = np.broadcast_to(commit[:, :, None, :], (N, 8, K, O)); dn = np.broadcast_to(done[:, :, None, :], (N, 8, K, O)).reshape(N, 8, 1, -1)
        d = np.where(cm.reshape(N, 8, 1, -1), got[twin], e)
        np.put_along_axis(v, np.where(cm, c, W).reshape(N, 8, 1, -1), d, 3)
        u = np.add.reduce(d.reshape(N, 8, 2, 8, K, O).astype(np.int64), axis=3); hs = (u[:, :, 0] * u[:, :, 1]) >> 3
        new = np.zeros((N, 8, K, O), np.int64); new[:, :, 0] = hs[:, :, 0] & (W - 1)
        for k in range(1, K): new[:, :, k] = (new[:, :, k - 1] + 1 + (hs[:, :, k] & (W // K - 1))) & (W - 1)
        c = np.where(done[:, :, None, :], new, c)
        e = np.where(dn, np.take_along_axis(v, c.reshape(N, 8, 1, -1), 3), e)
    lock[..., W] = 0
    mine = np.take_along_axis(lock, c.reshape(N, 8, -1), 2).reshape(N, 8, K, O) == own
    ys = np.add.reduce(v[..., :W] * np.arange(1, 17, dtype=np.int32).reshape(16, 1), axis=2)
    return {"ys": ys.astype(np.float32), "yc": np.stack([gtable(a.reshape(8, -1)) for a in c]).astype(np.float32),
            "yh": np.stack([gtable(a.reshape(8, -1)) for a in mine]).astype(np.float32), "yl": np.stack([gtable(a) for a in cur]).astype(np.float32)}

from concourse.mybir import dt, AluOpType, ActivationFunctionType

ALU = AluOpType
ACT = ActivationFunctionType
STEPS = 4
NV = 8192
EA, DUM, VO, EB = 0, 4096, 4352, 12544
BIGW = 16640
LW = 12416
HELD = 262144.0
CODE = 33
NVC = 3
WAKE, CY = 0.03, 0.00083
INORDER = ("g", "y")
URGE = {"rsf": 4.0}

SCRATCH = {
    "big": ("sbuf", [128, BIGW], "bfloat16"),
    "snk": ("sbuf", [128, 16, 256], "bfloat16"),
    "diff": ("sbuf", [128, 4096], "bfloat16"),
    "absd": ("sbuf", [128, 4096], "bfloat16"),
    "lock": ("sbuf", [128, LW], "float32"),
    "yt": ("sbuf", [128, 256 + NV], "float32"),
    "oh": ("sbuf", [128, 2048], "bfloat16"),
    "eq": ("sbuf", [128, 1920], "bfloat16"),
    "eqd": ("sbuf", [128, 256], "bfloat16"),
    "ld_": ("sbuf", [128, 2048], "bfloat16"),
    "lu_": ("sbuf", [128, 2048], "bfloat16"),
    "sel_": ("sbuf", [128, 2048], "bfloat16"),
}
for _n in ("csk", "hok", "keyi", "ci", "ti", "tj", "ui", "th", "tl_"):
    SCRATCH[_n] = ("sbuf", [128, 256], "int32")
for _n in ("r16", "jt1", "jt2", "dj", "kc8", "rst", "rbig", "diag", "tri", "key", "ka", "ue", "hf", "mx", "mkt", "cg", "cs2", "clm",
           "m1", "s1", "f1", "f2", "xab", "xcm", "xun", "xp", "xk", "xm", "pxx", "pd", "kx", "kd", "cv", "yco", "yho", "yd"):
    SCRATCH[_n] = ("sbuf", [128, 256], "float32")
SCRATCH["codec"] = ("sbuf", [128, 1024], "float32")
for _n in ("iw", "pw", "ldw"):
    SCRATCH[_n] = ("sbuf", [128, 296], "float32")
for _n in ("qb", "blkf"):
    SCRATCH[_n] = ("sbuf", [128, 128], "float32")
for _n in ("blk", "mix", "iotas", "ly", "id_", "nid_"):
    SCRATCH[_n] = ("sbuf", [128, 128], "bfloat16")
SCRATCH["ldg"] = ("sbuf", [128, 256], "bfloat16")
SCRATCH["chl"] = ("sbuf", [128, 512], "bfloat16")
for _n in ("coff", "loff", "eidx", "ku"):
    SCRATCH[_n] = ("sbuf", [128, 256], "uint16")
for _n in ("xu", "ou", "curu", "curv", "offu", "listu"):
    SCRATCH[_n] = ("sbuf", [128, 16], "uint16")
FS = ["prf", "pgf", "wu", "gi", "giu", "q8", "sent", "home", "j16", "one", "thr", "fulls", "nb", "x", "dec", "decm", "val", "byc",
      "p", "p8", "gone", "isb", "mv", "d1", "c1", "d2", "cura", "curb", "fr", "cl", "k1", "k2", "lose", "offl", "l1", "l2", "yl"]
IS = ["mki", "xl", "cint", "o", "ep", "pint", "by", "xx", "aw0", "aw1", "aw2", "aw3", "h0", "pr", "pg", "wk"]
SCRATCH["fs"] = ("sbuf", [128, 16 * len(FS)], "float32")
SCRATCH["is_"] = ("sbuf", [128, 16 * len(IS)], "int32")
for _n in ("rdy", "rs", "sfu", "lfu"):
    SCRATCH[_n] = ("sbuf", [128, 16], "bfloat16")
for _t in range(STEPS):
    SCRATCH["sf%d" % _t] = ("sbuf", [128, 16], "bfloat16")
    SCRATCH["lsf%d" % _t] = ("sbuf", [128, 16], "bfloat16")
    SCRATCH["skg%d" % _t] = ("sbuf", [128, 256], "float32")
    SCRATCH["lkc%d" % _t] = ("sbuf", [128, 256], "float32")
    SCRATCH["snd%d" % _t] = ("sbuf", [128, 256], "bfloat16")
    SCRATCH["lnd%d" % _t] = ("sbuf", [128, 256], "bfloat16")
for _b in range(8):
    SCRATCH["b%d" % _b] = ("psum", [128, 512], "float32")

SEMAPHORES = ["c" + q for q in "vspgy"] + ["dcs", "dho", "dwk", "dsn", "dx0", "dx1", "oys", "oyc", "oyh", "oyl", "rfu", "qfu"]
for _t in range(STEPS):
    SEMAPHORES += [k + str(_t) for k in ("rsf", "rkc", "rdd", "qsf", "qkc", "qdd")]


def emitter(g, T):
    eng = {"v": g.vector, "s": g.scalar, "p": g.tensor, "g": g, "y": g.sync}
    known = {q: {} for q in eng}
    cnt = {q: 0 for q in eng}
    hist, bank, final, prog = {}, {}, {}, []

    def isbank(n):
        return n[0] == "b" and n[1:].isdigit()

    def before(q, rd, wr):
        evs = []
        for isw, regs in ((False, rd), (True, wr)):
            for n, a, b in regs:
                if isbank(n):
                    evs += [e for q2, e in bank.get(n, {}).items() if q2 != q]
                for lo, hi, w, q2, asyn, e in hist.get(n, ()):
                    if lo < b and hi > a and (w or isw) and not (q2 == q == "p"):
                        evs.append(e)
        todo = {}
        for s, v, ck in evs:
            if known[q].get(s, 0) < v and (s not in todo or todo[s][0] < v):
                todo[s] = (v, ck)
        for s in sorted(todo):
            v = todo[s][0]
            if not any(s2 != s and c2.get(s, 0) >= v for s2, (v2, c2) in todo.items()):
                eng[q].wait_ge(T.sem[s], v)
        for s, (v, ck) in todo.items():
            for s2, v2 in ck.items():
                known[q][s2] = max(known[q].get(s2, 0), v2)

    def after(q, rd, wr, sem, val, asyn):
        ck = dict(known[q])
        ck[sem] = val
        e = (sem, val, ck)
        final[sem] = val
        for n, a, b in wr:
            hist[n] = [x for x in hist.get(n, ()) if not (a <= x[0] and x[1] <= b)] + [(a, b, True, q, asyn, e)]
        for n, a, b in rd:
            hist[n] = [x for x in hist.get(n, ()) if not (not x[2] and x[3] == q and not asyn and a <= x[0] and x[1] <= b)] + [(a, b, False, q, asyn, e)]
        for n, a, b in rd + wr:
            if isbank(n):
                bank.setdefault(n, {})[q] = e

    def op(q, call, outs, ins, cost):
        prog.append((q, "op", call, [x for o in ins for x in o[1]], [x for o in outs for x in o[1]], cost, cost, None))

    def dma(q, out, in_, sem, lat):
        call = lambda: eng[q].dma_start(out=out[0], in_=in_[0]).then_inc(T.sem[sem], 16)
        prog.append((q, "dma", call, in_[1], out[1], 0.1, lat, sem))

    def send(topo, core, dst, out, in_, rsem, lsem):
        rid, pid, _s = topo.addr(dst)
        n = len(topo.engines(core, dst))
        call = lambda: g.remote_dma(out[0], in_[0], T.sem[rsem], T.sem[lsem], pid, rid, topo.mask(core, dst))
        prog.append(("g", "send", call, in_[1], [], 0.6, 2.0, (lsem, n)))
        prog.append(("net", "land", None, in_[1], out[1], 0.0, 3.0, (rsem, n)))

    def order():
        m = len(prog)
        succ, npred, seen = [[] for _ in range(m)], [0] * m, {}
        for i, (q, kind, call, rd, wr, occ, lat, x) in enumerate(prog):
            pred = {}
            for isw, regs in ((False, rd), (True, wr)):
                for n, a, b in regs:
                    bk = isbank(n)
                    for k, lo, hi, w, q2 in seen.get(n, ()):
                        if k != i and ((lo < b and hi > a and (w or isw)) or (bk and (q2 != q or q == "p"))):
                            pred[k] = 1
            for n, a, b in wr:
                keep = [e for e in seen.get(n, ()) if not (a <= e[1] and e[2] <= b) or isbank(n)]
                seen[n] = keep[-60:] + [(i, a, b, True, q)]
            for n, a, b in rd:
                seen.setdefault(n, []).append((i, a, b, False, q))
            npred[i] = len(pred)
            for k in pred:
                succ[k].append(i)

        def wake(i, k):
            return 0.0 if prog[i][0] == prog[k][0] == "p" else WAKE

        way = [0.0] * m
        for i in range(m - 1, -1, -1):
            way[i] = prog[i][6] + max([way[k] + wake(i, k) for k in succ[i]] + [0.0])
            if prog[i][1] == "land":
                way[i] += URGE.get(prog[i][7][0][:3], 0.0)
        when, free, ready, out = [0.0] * m, {}, {}, []
        for i in range(m):
            if npred[i] == 0:
                ready.setdefault(prog[i][0], []).append(i)
        while len(out) < m:
            best = None
            for q in ready:
                if not ready[q]:
                    continue
                if q == "net":
                    i = min(ready[q], key=lambda i: when[i])
                    t = when[i]
                elif q in INORDER:
                    i = min(ready[q])
                    t = max(free.get(q, 0.0), when[i])
                else:
                    t = max(free.get(q, 0.0), min(when[i] for i in ready[q]))
                    i = max((i for i in ready[q] if when[i] <= t + 0.001), key=lambda i: way[i])
                if best is None or t < best[0]:
                    best = (t, q, i)
            t, q, i = best
            ready[q].remove(i)
            out.append(i)
            if q != "net":
                free[q] = t + prog[i][5]
            for k in succ[i]:
                when[k] = max(when[k], t + prog[i][6] + wake(i, k))
                npred[k] -= 1
                if npred[k] == 0:
                    ready.setdefault(prog[k][0], []).append(k)
        return out

    def issue():
        for i in order():
            q, kind, call, rd, wr, occ, lat, x = prog[i]
            if kind == "land":
                final[x[0]] = x[1]
                nm, a, b = wr[0]
                hist[nm] = [(a, b, True, "net", True, (x[0], x[1], {x[0]: x[1]}))]
                continue
            before(q, rd, wr)
            if kind == "op":
                cnt[q] += 1
                call().then_inc(T.sem["c" + q], 1)
                after(q, rd, wr, "c" + q, cnt[q], False)
            else:
                call()
                s, n = (x, 16) if kind == "dma" else x
                after(q, rd, wr, s, n, True)
        for s in sorted(final):
            if known["g"].get(s, 0) < final[s]:
                g.wait_ge(T.sem[s], final[s])

    return op, dma, send, issue


def rank_program(g, core, T, topo):
    rank = T.rank_of(core)
    if rank is None:
        return
    op, dma, send, issue = emitter(g, T)

    def r(n, a=None, b=None, st=None):
        a = 0 if a is None else a
        b = T[n].shape[-1] if b is None else b
        return (T[n][:, a:b] if st is None else T[n][:, a:b:st], [(n, a, b)], -((a - b) // (st or 1)))

    def f(n, k=16):
        i = 16 * FS.index(n)
        return r("fs", i, i + k)

    def iv(n, k=16):
        i = 16 * IS.index(n)
        return r("is_", i, i + k)

    def ind(win, off):
        return (win[0].indirect(off[0]), win[1] + off[1], 16 * off[2])

    def hd(n):
        return r(n, 0, 256, 16)

    def tl(n):
        return r(n, 15, 256, 16)

    def ext(t):
        return (t, [], 0)

    def kind(o):
        w, _s, d = SCRATCH[o[1][0][0]]
        return len(o[1]) > 1, w == "psum", d in ("bfloat16", "uint16")

    def cost(out, a, b=None):
        n, ko, ka = a[2], kind(out), kind(a)
        if ko[0]:
            return 0.05 + n * 3.8 * CY
        if ka[0]:
            return 0.05 + n * 1.5 * CY
        if b is not None:
            return max(64, n * (1 if ka[1] or kind(b)[1] else 2)) * CY
        return max(64, n * (0.5 if ko[2] and ka[2] else 1)) * CY

    def tt(out, a, b, o):
        op("v", lambda: g.vector.tensor_tensor(out=out[0], in0=a[0], in1=b[0], op=o), [out], [a, b], cost(out, a, b))

    def ts(out, a, s1, s2, o0, o1=None):
        ins = [a] + [s for s in (s1, s2) if isinstance(s, tuple)]
        x1 = s1[0] if isinstance(s1, tuple) else s1
        if o1 is None:
            op("v", lambda: g.vector.tensor_scalar(out=out[0], in0=a[0], scalar1=x1, scalar2=None, op0=o0), [out], ins, cost(out, a))
        else:
            op("v", lambda: g.vector.tensor_scalar(out=out[0], in0=a[0], scalar1=x1, scalar2=s2, op0=o0, op1=o1), [out], ins, cost(out, a))

    def cp(out, a):
        op("v", lambda: g.vector.tensor_copy(out=out[0], in_=a[0]), [out], [a], cost(out, a))

    def scan(out, d0, d1, o0, o1):
        op("v", lambda: g.vector.tensor_tensor_scan(out=out[0], data0=d0[0], data1=d1[0], initial=0.0, op0=o0, op1=o1), [out], [d0, d1],
           max(64, d1[2]) * CY)

    def ms(out, v):
        op("v", lambda: g.vector.memset(out[0], v), [out], [], cost(out, out))

    def act(out, a, fn, bias=0.0, scale=1.0):
        cs = cost(out, a) if kind(out)[0] or kind(a)[0] else max(64, a[2]) * CY
        if bias == 0.0 and scale == 1.0:
            op("s", lambda: g.scalar.activation(out=out[0], in_=a[0], func=fn), [out], [a], cs)
        else:
            op("s", lambda: g.scalar.activation(out=out[0], in_=a[0], func=fn, bias=bias, scale=scale), [out], [a], cs)

    def mm(out, l, x, start, stop):
        op("p", lambda: g.tensor.matmul(out[0], l[0], x[0], start, stop), [out], [l, x], max(64, x[2]) * CY * (1 if kind(x)[2] else 4))

    def iota(out, pat, base, cm):
        op("g", lambda: g.iota(out[0], pat, base, cm, allow_small_or_imprecise_dtypes=True), [out], [], 0.13 + 2 * CY * out[2])

    def tell(t, out, in_, rsem, lsem):
        send(topo, core, T.cores[rank ^ (1 + t)], r(out), r(in_), rsem, lsem)

    add, sub, mul, mx, mn = ALU.add, ALU.subtract, ALU.mult, ALU.max, ALU.min
    band, shr = ALU.bitwise_and, ALU.arith_shift_right

    dma("s", r("csk"), ext(T.cs[:]), "dcs", 2.5)
    dma("y", r("hok"), ext(T.hold[:]), "dho", 3.0)
    dma("s", iv("wk"), ext(T.wake[:]), "dwk", 2.5)
    dma("y", (T.snk[:], [("snk", 0, 256)], 256), ext(T.snap[:]), "dsn", 8.0)
    dma("s", r("big", VO, VO + 4096), ext(T.x[:, 0:4096]), "dx0", 13.0)
    dma("y", r("big", VO + 4096, EB), ext(T.x[:, 4096:8192]), "dx1", 14.0)

    iota(iv("pr", 1), [[0, 1]], 0, 1)
    iota(r("r16"), [[0, 16], [1, 16]], 0, 0)
    iota(f("q8", 8), [[1, 8]], 0, 0)
    iota(r("dj"), [[16, 256]], 8192, 1)
    iota(r("qb"), [[1, 8], [0, 16]], 0, 0)
    iota(f("j16"), [[16, 16]], 0, 0)
    iota(r("kc8"), [[0, 16], [8192, 16]], 8192, 0)

    def codes(a):
        iota(r("yt", 256 + 1024 * a, 1280 + 1024 * a), [[16, 4], [0, 16], [1, 16]], CODE + 64 * a, 0)

    codes(0)
    iota(r("lock", 5120, 8192), [[0, 3072]], 0, 0)
    codes(1)
    iota(f("sent"), [[16, 16]], 8192, 1)

    ms(r("sel_"), 0.0)
    for a, n in ((0, 2048), (2048, 2048), (4096, 1024)):
        act(r("lock", a, a + n), r("sel_", 0, n), ACT.Copy)
    for n in ("xab", "xcm", "xun", "xp", "xk", "xm", "pw", "ldw"):
        act(r(n), r("sel_", 0, T[n].shape[-1]), ACT.Copy)
    ms(r("ld_"), 0.0)
    ts(iv("pg", 1), iv("pr", 1), 4, None, shr)
    cp(f("pgf", 1), iv("pg", 1))
    ts(iv("h0", 1), iv("pr", 1), 15, None, band)
    cp(f("prf", 1), iv("h0", 1))
    PRF, PGF = f("prf", 1), f("pgf", 1)
    ts(f("gi", 8), f("q8", 8), PGF, None, ALU.is_equal)
    ms(f("one"), 1.0)
    gi, giu = 16 * FS.index("gi"), 16 * FS.index("giu")
    for k in range(16):
        cp(r("ci", k, 256, 16), r("csk", 16 * k, 16 * k + 16))
    cp(r("coff"), r("ci"))
    UNDX, T1, T2, DG = r("b6", 0, 256), r("b6", 256, 512), r("b7", 0, 256), r("b7", 256, 512)

    def chl():
        ts(r("th"), r("ci"), 7, None, shr)
        ts(r("tl_"), r("ci"), 127, None, band)
        ts(r("chl", 0, 512, 2), r("th"), 128.0, 256.0, mul, add)
        cp(r("chl", 1, 512, 2), r("tl_"))

    for h in range(8):
        ts(r("ld_", 16 * h, 2048, 129), f("one"), r("fs", gi + h, gi + h + 1), None, mul)
    ms(r("lu_"), 0.0)
    ts(f("wu", 1), PRF, 8.0, 4095.0, ALU.is_lt, mul)
    ts(f("wu", 1), f("wu", 1), 1.0, None, add)
    ts(f("giu", 8), f("gi", 8), f("wu", 1), None, mul)
    for h in range(8):
        ts(r("lu_", 16 * h, 2048, 129), f("one"), r("fs", giu + h, giu + h + 1), None, mul)
    ts(r("diag"), r("r16"), PRF, None, ALU.is_equal)
    ts(r("blk"), r("qb"), PGF, None, ALU.is_equal)
    ts(r("blkf"), r("qb"), PGF, None, ALU.is_equal)
    ts(r("tri"), r("r16"), PRF, None, ALU.is_gt)
    tt(r("f1", 0, 128), r("blkf"), r("tri", 0, 128), mul)
    tt(r("f1", 128, 256), r("blkf"), r("diag", 0, 128), mul)
    cp(r("id_"), r("f1", 128, 256))
    ts(r("nid_"), r("f1", 128, 256), -1.0, None, mul)
    ts(r("f1", 128, 256), r("f1", 128, 256), -64.0, None, mul)
    tt(r("f2", 0, 128), r("f1", 0, 128), r("f1", 128, 256), add)
    tt(r("mix"), r("f2", 0, 128), r("blkf"), sub)
    ts(r("f2", 128, 256), r("r16", 0, 128), 936.0, None, add)
    tt(r("f1", 0, 128), r("f2", 128, 256), r("blkf"), mul)
    ts(r("iotas"), r("f1", 0, 128), -1000.0, None, add)
    ts(f("wu", 1), PRF, 1.0, None, add)
    ts(r("ly"), r("blkf"), f("wu", 1), None, mul)
    ts(f("j16"), f("j16"), PRF, None, add)
    chl()
    ms(r("big", DUM, VO), 0.0)

    for k in range(16):
        cp(r("hf", k, 256, 16), r("hok", 16 * k, 16 * k + 16))
    tt(r("f2"), r("ci"), r("dj"), sub)
    tt(r("f2"), r("f2"), r("hf"), mul)
    tt(r("f2"), r("f2"), r("dj"), add)
    cp(r("loff"), r("f2"))

    def locks(a):
        for b in (2 * a, 2 * a + 1):
            act(ind(r("lock"), r("loff", 32 * b, 32 * b + 32)), r("yt", 256 + 512 * b, 768 + 512 * b), ACT.Silu)

    def pre_a():
        scan(r("mkt"), r("rbig"), r("key"), mx, mn)
        ts(f("fulls"), tl("mkt"), HELD, 1.0, ALU.is_ge, add)
        cp(iv("mki"), tl("mkt"))
        ts(iv("xl"), iv("mki"), 8191, None, band)
        cp(r("xu"), iv("xl"))

    ts(r("rst"), r("r16"), 0.0, None, ALU.is_gt)
    ts(r("rbig"), r("r16"), 0.0, 1048576.0, ALU.is_equal, mul)
    tt(r("f1"), r("ci"), r("kc8"), add)
    ts(r("f2"), r("hf"), HELD, None, mul)
    tt(r("key"), r("f1"), r("f2"), add)
    pre_a()
    cp(r("sfu"), f("fulls"))
    tell(0, "lfu", "sfu", "rfu", "qfu")
    locks(0)
    locks(1)
    for oc in range(16):
        cp(r("big", EA + 256 * oc, EA + 256 * oc + 256), (T.snk[:, :, 16 * oc:16 * oc + 16], [("snk", 0, 256)], 256))

    codes(2)
    codes(3)
    iota(r("jt1"), [[16, 256]], EA - VO, 0)
    iota(r("jt2"), [[16, 256]], EB - VO, 0)
    iota(r("iw"), [[1, 296]], 0, 0)
    iota(r("codec"), [[512, 4], [1, 256]], CODE + 512, 0)

    for h in range(8):
        ts(r("sel_", 16 * h, 2048, 129), r("diag", 0, 16), r("fs", gi + h, gi + h + 1), None, mul)
    ts(f("home"), f("j16"), float(CODE), None, add)
    cp(f("cura"), f("home"))
    cp(r("curu"), f("home"))
    cp(DG, r("diag"))
    ms(r("ldw", 0, 8), 100.0)
    for t in range(STEPS):
        ts(iv("aw%d" % t), iv("wk"), t, 1, shr, band)

    def constants3():
        ts(r("jt1"), r("jt1"), PRF, None, add)
        ts(r("jt2"), r("jt2"), PRF, None, add)
        ts(r("f2"), r("diag"), 1000000.0, -1.0, mul, add)
        for t in range(STEPS):
            tt(r("codec", 256 * t, 256 * t + 256), r("codec", 256 * t, 256 * t + 256), r("f2"), mn)

    V = r("big", VO, EB)
    VD = r("big", DUM, EB)
    esrc = [EA, EA, EB, EA]

    def sums(bk, lw, src, base, a):
        for m in range(16):
            mm(r(bk, 64 * a, 64 * a + 64), r(lw, 128 * m, 128 * m + 128), r(src, base + 1024 * a + m, base + 1024 * a + 1024, 16), m == 0, m == 15)

    def dist(a):
        sums("b0", "ld_", "absd", 0, a)

    def halves(a):
        sums("b1", "lu_", "diff", 0, a)

    def chain(out):
        ts(r("ti"), r("ui"), 12, None, shr)
        ts(r("tj"), r("ui"), 4095, None, band)
        tt(r("ti"), r("ti"), r("tj"), mul)
        ts(r("tj"), r("ti"), 3, 511, shr, band)
        ts(iv("h0"), hd("ti"), 3, 8191, shr, band)
        ts(r("hf"), r("tj"), 8193.0, None, add)
        ts(hd("hf"), iv("h0"), 8192.0, None, add)
        scan(out, r("rst"), r("hf"), mul, add)

    def judge_v(a, t):
        d = r("diff", 1024 * a, 1024 * a + 1024)
        tt(d, ind(V, r("coff", 64 * a, 64 * a + 64)), r("big", esrc[t] + 1024 * a, esrc[t] + 1024 * a + 1024), sub)
        act(r("absd", 1024 * a, 1024 * a + 1024), d, ACT.Abs)

    def judge_s(a, t):
        act(r("diff", 1024 * a, 1024 * a + 1024), ind(V, r("coff", 64 * a, 64 * a + 64)), ACT.Copy)
        for h, bk in ((0, "b2"), (1, "b3")):
            c = 1024 * a + 512 * h
            mm(r(bk), r("id_"), r("diff", c, c + 512), True, False)
            mm(r(bk), r("nid_"), r("big", esrc[t] + c, esrc[t] + c + 512), False, True)
            act(r("absd", c, c + 512), r(bk), ACT.Abs)

    def pre_b():
        tt(r("cg"), ind(r("lock", 0, NV), r("xu")), r("diag"), mul)
        scan(r("cs2"), r("rst"), r("cg"), mul, add)
        cp(iv("cint"), tl("cs2"))
        ts(iv("o"), iv("cint"), 511, None, band)
        cp(r("ou"), iv("o"))
        act(r("ldg"), ind(r("ldw"), r("ou")), ACT.Copy)
        ts(iv("ep"), iv("cint"), 9, None, shr)

    def pre_c():
        for m in range(16):
            mm(r("b5", 256, 272), r("sel_", 128 * m, 128 * m + 128), r("ldg", m, 256, 16), m == 0, m == 15)
        tt(f("val"), iv("ep"), r("b5", 256, 272), ALU.is_ge)
        tt(f("byc"), f("val"), iv("o"), mul)
        ts(f("p8"), f("byc"), 8192.0, None, mul)
        tt(f("p"), f("p8"), iv("xl"), add)

    def lanes(t):
        cur, curn = ("cura", "curb") if t % 2 == 0 else ("curb", "cura")
        cu, cun = ("curu", "curv") if t % 2 == 0 else ("curv", "curu")
        last = t == STEPS - 1
        ts(f("decm"), f("dec"), -8388609.0, 8388608.0, mul, add)
        tt(hd("xp"), f("p"), f("decm"), mn)
        scan(r("pxx"), r("rst"), r("xp"), mul, add)
        tt(r("pd"), r("pxx"), DG, mul)
        mm(r("b4", 0, 256), r("blkf"), r("pd"), True, True)
        act(r("pw", CODE, CODE + 256), r("b4", 0, 256), ACT.Copy)
        if not last:
            act(r("b4", 0, 256), r("pw", CODE, CODE + 256), ACT.Relu, scale=-float(t + 1))
        act(r("cv"), ind(r("iw"), r(cu)), ACT.Identity, bias=float(512 * (t + 1)))
        tt(r("cg"), ind(r("pw"), r(cu)), r("diag"), mul)
        scan(r("cs2"), r("rst"), r("cg"), mul, add)
        cp(iv("pint"), tl("cs2"))
        ts(iv("by"), iv("pint"), 13, None, shr)
        ts(iv("xx"), iv("pint"), 8191, None, band)
        ts(f("fr"), iv("by"), 0.0, None, ALU.is_equal)
        tt(f("k1"), iv("xx"), f("sent"), sub)
        tt(f("cl"), f("fr"), iv("aw%d" % t), mul)
        tt(f("k1"), f("k1"), f("cl"), mul)
        tt(hd("xk"), f("k1"), f("sent"), add)
        scan(r("kx"), r("rst"), r("xk"), mul, add)
        if not last:
            tt(r("ldw", CODE, CODE + 256), r("ldw", CODE, CODE + 256), r("b4", 0, 256), mx)
        tt(r("kd"), r("kx"), DG, mul)
        mm(r("b4", 256, 512), r("blkf"), r("kd"), True, True)
        ts(f("isb"), iv("by"), 0.0, None, ALU.is_gt)
        tt(f("d1"), iv("by"), f(cur), sub)
        tt(f("mv"), f("isb"), iv("aw%d" % t), mul)
        ts(f("gone"), iv("by"), 0.0, None, ALU.is_lt)
        tt(f("d1"), f("d1"), f("mv"), mul)
        tt(f("c1"), f(cur), f("d1"), add)
        tt(f("d2"), f("home"), f("c1"), sub)
        tt(f("d2"), f("d2"), f("gone"), mul)
        tt(f(curn), f("c1"), f("d2"), add)
        cp(r(cun), f(curn))
        tt(T2, r("kx"), r("b4", 256, 512), ALU.is_equal)
        cp(r("ku"), r("b4", 256, 512))
        tt(r("eqd"), T2, r("tri"), mul)
        mm(r("b5", 0, 256), r("blk"), r("eqd"), True, False)
        at = 0
        for oc in range(15):
            n = 240 - 16 * oc
            ts(r("eq", at, at + n), r("ku", 256 - n, 256), r("kx", 16 * oc, 16 * oc + 1), None, ALU.is_equal)
            mm(r("b5", 256 - n, 256), r("blk"), r("eq", at, at + n), False, oc == 14)
            at += n
        tt(f("k2"), f("sent"), hd("xk"), sub)
        tt(r("cg"), r("b5", 0, 256), r("diag"), mul)
        scan(r("cs2"), r("rst"), r("cg"), mul, add)
        ts(f("lose"), tl("cs2"), 0.0, None, ALU.is_gt)
        tt(f("k2"), f("k2"), f("lose"), mul)
        tt(f("offl"), hd("xk"), f("k2"), add)
        cp(r("offu"), f("offl"))
        cp(ind(r("lock"), r("offu")), r("cv"))
        tt(r("clm"), ind(r("lock", 0, NV), r("xu")), r("codec", 256 * t, 256 * t + 256), ALU.is_equal)
        scan(r("cs2"), r("rst"), r("clm"), mul, add)
        tt(hd("xm"), tl("mkt"), tl("cs2"), mul)
        scan(T1, r("rst"), r("xm"), mul, add)
        tt(T2, r("keyi"), T1, ALU.is_equal)
        if not last:
            ts(T1, T2, HELD, None, mul)
            tt(r("key"), r("keyi"), T1, add)
            pre_a()

    def decide(t):
        if t == 0:
            tt(f("l1"), f("nb"), f("fulls"), mul)
            tt(f("l2"), f("l1"), r("lfu"), mul)
            tt(f("x"), f("l2"), r("lsf0"), mul)
        else:
            tt(f("x"), r("sf%d" % t), r("lsf%d" % t), mul)
        ts(r("rdy"), f("x"), 4.0, None, ALU.is_equal)
        scan(r("rs"), f("one"), r("rdy"), mul, add)
        mm(r("b2", 0, 16), r("mix"), r("rdy"), True, False)
        mm(r("b2", 0, 16), r("blk"), r("rs"), False, True)
        ts(hd("xab"), f("x"), 0.0, None, ALU.is_equal)
        for oc in range(16):
            ts(r("oh", 128 * oc, 128 * oc + 128), r("iotas"), r("b2", oc, oc + 1), None, ALU.is_equal)
            mm(r("b3", 0, 32), r("oh", 128 * oc, 128 * oc + 128), r("chl", 32 * oc, 32 * oc + 32), oc == 0, oc == 15)
        ts(hd("xcm"), r("b2", 0, 16), -48.0, None, ALU.is_lt)
        tt(f("dec"), hd("xab"), hd("xcm"), add)
        ts(f("thr"), f("dec"), 1000000.0, 320.0, mul, add)
        ts(hd("xun"), f("dec"), -1.0, 1.0, mul, add)
        tt(f("l1"), r("b3", 0, 32, 2), f("j16"), mx)
        tt(f("l2"), r("b3", 1, 32, 2), f("l1"), add)
        cp(r("listu"), f("l2"))
        cp(r("snd%d" % t), ind(VD, r("listu")))
        tell(t, "lnd%d" % t, "snd%d" % t, "rdd%d" % t, "qdd%d" % t)

    def ysum(c):
        bk = "b%d" % (c % 2)
        mm(r(bk), r("ly"), r("big", VO + 512 * c, VO + 512 * c + 512), True, True)
        act(r("yt", 256 + 512 * c, 768 + 512 * c), r(bk), ACT.Copy)

    nc = 64 * NVC
    for t in range(STEPS):
        last = t == STEPS - 1
        if t == 0:
            for a in range(4):
                sums("b4", "lu_", "big", EA, a)
            for a in range(4):
                judge_v(a, t)
                dist(a)
                if a < 2:
                    halves(a)
            halves(2)
            halves(3)
            ms(f("thr"), 320.0)
        else:
            chl()
            for a in range(NVC, 4):
                judge_s(a, t)
            for a in range(NVC):
                judge_v(a, t)
                dist(a)
            for a in range(NVC, 4):
                dist(a)
            for a in range(4):
                halves(a)
        scan(r("mx"), r("rst"), r("b0", 0, 256), mul, mx)
        tt(f("nb"), f("thr"), tl("mx"), ALU.is_ge)
        if t == 0:
            cp(r("sf0"), f("nb"))
            locks(2)
            locks(3)
        else:
            tt(r("sf%d" % t), f("nb"), f("fulls"), mul)
        tell(t, "lsf%d" % t, "sf%d" % t, "rsf%d" % t, "qsf%d" % t)
        if t in (1, 2):
            e0, e1 = (EA, EB) if t == 1 else (EB, EA)
            lo, hi = (EA, EB) if t == 1 else (VO, EB + 4096)
            tt(r("f1"), r("jt%d" % t), r("ci"), sub)
            tt(T1, r("f1"), UNDX, mul)
            tt(r("f1"), T1, r("ci"), add)
            ts(r("eidx"), r("f1"), float(VO - lo), None, add)
            for a in range(4):
                act(r("big", e1 + 1024 * a, e1 + 1024 * a + 1024), ind(r("big", lo, hi), r("eidx", 64 * a, 64 * a + 64)), ACT.Copy)
        if t > 0:
            pre_b()
        kg = r("skg%d" % t)
        if t == 0:
            cp(r("ue"), r("b4", 0, 256))
            tt(r("ui"), r("b1", 0, 256), r("ue"), add)
        else:
            tt(r("ui", 0, nc), r("b1", 0, nc), r("ue", 0, nc), add)
            cp(r("ui", nc, 256), r("b1", nc, 256))
        chain(kg)
        tell(t, "lkc%d" % t, "skg%d" % t, "rkc%d" % t, "qkc%d" % t)
        if t == 0:
            cp(r("ui"), r("ue"))
            chain(r("ka"))
            constants3()
        else:
            tt(r("f2"), r("ka"), kg, sub)
            tt(T1, r("f2"), UNDX, mul)
            tt(r("ka"), T1, kg, add)
            pre_c()
        if last:
            for c in range(4):
                ysum(c)
        decide(t)
        if t in (1, 2):
            for a in range(NVC):
                sums("b1", "lu_", "big", e1, a)
            act(r("ue", 0, nc), r("b1", 0, nc), ACT.Copy)
        if last:
            for c in range(4, 11):
                ysum(c)
        scan(UNDX, r("rst"), r("xun"), mul, add)
        tt(r("m1"), r("key"), UNDX, mul)
        scan(T1, r("rst"), r("xab"), mul, add)
        tt(T1, r("ka"), T1, mul)
        tt(r("s1"), r("m1"), T1, add)
        scan(T2, r("rst"), r("xcm"), mul, add)
        tt(T2, r("lkc%d" % t), T2, mul)
        tt(r("keyi"), r("s1"), T2, add)
        ts(r("ci"), r("keyi"), 8191, None, band)
        if not last:
            cp(r("coff"), r("ci"))
            cp(ind(VD, r("listu")), r("lnd%d" % t))
        if t == 0:
            pre_b()
            pre_c()
        lanes(t)
    for c in range(11, 16):
        ysum(c)
    mm(r("b2", 0, 256), r("ly"), r("lnd3"), True, True)
    act(r("yd"), r("b2", 0, 256), ACT.Copy)
    cp(ind(r("yt"), r("listu")), r("yd"))
    dma("y", ext(T.ys[:]), (T.yt[0:128:16, 256:256 + NV], [("yt", 256, 256 + NV)], 0), "oys", 4.0)
    ts(f("yl"), f("cura"), -float(CODE), None, add)
    dma("y", ext(T.yl[:]), f("yl"), "oyl", 2.0)
    for k in range(16):
        cp(r("yco", 16 * k, 16 * k + 16), r("ci", k, 256, 16))
    dma("y", ext(T.yc[:]), r("yco"), "oyc", 2.0)
    ts(r("f1"), r("keyi"), HELD, None, ALU.is_ge)
    for k in range(16):
        tt(r("yho", 16 * k, 16 * k + 16), (T.b7[:, k:256:16], T2[1], 16), r("f1", k, 256, 16), add)
    dma("y", ext(T.yh[:]), r("yho"), "oyh", 2.0)
    issue()
